import numpy as np
CORES = [24,25,26,27,28,29,30,31,224,225,226,227,228,229,230,231]
N = 16
B, S = 16, 16
def entries(a): return a.T.reshape(-1)
def pack(v, P): return np.ascontiguousarray(np.asarray(v, np.int32).reshape(-1, P).T)
def lists(rng, how):
    Q = rng.integers(0, N * B, N * B)
    if how == "alike": Q[:] = rng.integers(N * B)
    if how == "stay": Q = np.arange(N * B)
    if how == "distinct": Q = rng.permutation(N * B)
    if how == "hotrank": Q = B * int(rng.integers(N)) + rng.integers(0, B, N * B)
    if how == "swap": s = int(rng.integers(1, N)); Q = np.concatenate([B * ((r + s) % N) + rng.permutation(B) for r in range(N)])
    return {"parent": np.broadcast_to(pack(Q, 16), (N, 16, N * B // 16)).copy()}
def setup_inputs(rng):
    return dict({"c": rng.standard_normal((N, 128, B * S), dtype=np.float32)}, **lists(rng, "uniform"))
def setup_inputs_alike(rng):
    d = setup_inputs(rng); d.update(lists(rng, "alike"))
    for k in ("c",): d[k] = (d[k].astype(np.float32) * 1048576.0).astype(d[k].dtype)
    return d
def setup_inputs_distinct(rng):
    d = setup_inputs(rng); d.update(lists(rng, "distinct"))
    for k in ("c",): d[k] = (d[k].astype(np.float32) * (1 / 1024.0)).astype(d[k].dtype)
    return d
def setup_inputs_hotrank(rng):
    d = setup_inputs(rng); d.update(lists(rng, "hotrank"))
    return d
def setup_inputs_stay(rng):
    d = setup_inputs(rng); d.update(lists(rng, "stay"))
    return d
def setup_inputs_swap(rng):
    d = setup_inputs(rng); d.update(lists(rng, "swap"))
    return d
def check_inputs(x):
    bad = []
    if x["parent"].min() < 0 or x["parent"].max() >= N * B: bad.append("parent out of range")
    if not all(np.array_equal(a, x["parent"][0]) for a in x["parent"]): bad.append("parent isn't alike on all ranks")
    return bad
def reference(c, parent):
    A = np.concatenate(list(c), axis=1).reshape(128, N * B, S)
    Y = A[:, entries(parent[0]), :]
    return {"y": np.stack([Y[:, B * r:B * r + B].reshape(128, B * S) for r in range(N)])}

@@ -1,0 +1,245 @@
+from concourse.bass import DstId, RemoteDMATransfer
+from concourse.mybir import AluOpType
+
+MODE = "direct"
+NB, NCOL = 16, 16
+NS = 2
+W = NCOL // NS
+SW = NB * W
+
+SCRATCH = {
+    "cb": ("sbuf", [128, NB * NCOL], "float32"),
+    "st": ("sbuf", [128, NB * NCOL], "float32"),
+    "win": ("sbuf", [128, 8 * SW], "float32"),
+    "sel": ("sbuf", [128, 4 * SW], "float32"),
+    "win2": ("sbuf", [128, 2 * NB * NCOL], "float32"),
+    "yb": ("sbuf", [128, NB * NCOL], "float32"),
+    "rel": ("sbuf", [128, 2 * SW], "float32"),
+    "par": ("sbuf", [128, 16], "int32"),
+    "ki": ("sbuf", [128, 32], "int32"),
+    "kf": ("sbuf", [128, 32], "float32"),
+    "kt": ("sbuf", [128, 32], "float32"),
+    "k16": ("sbuf", [128, 16], "uint16"),
+    "pm": ("sbuf", [128, 16], "int32"),
+    "ph": ("sbuf", [128, 16], "int32"),
+    "pb": ("sbuf", [128, 16], "int32"),
+    "of1": ("sbuf", [128, 16 * W], "uint16"),
+    "tc": ("sbuf", [128, 1], "float32"),
+    "yy": ("sbuf", [128, 32], "float32"),
+    "yt": ("sbuf", [128, 32], "float32"),
+    "of2": ("sbuf", [128, 16], "uint16"),
+}
+SEMAPHORES = ["ldc", "ldp", "cst", "v", "dei", "sa", "sb", "a1", "a2", "ar", "ls", "fin", "sto"]
+
+
+def _bits(m):
+    return [e for e in range(16) if (m >> e) & 1]
+
+
+def _mask(es):
+    return sum(1 << e for e in es)
+
+
+def _chips(T, topo):
+    chips = []
+    for c in T.cores:
+        key = (topo.host(c), topo.chip(c))
+        hit = [ch for ch in chips if ch[0] == key]
+        if hit:
+            hit[0][1].append(c)
+        else:
+            chips.append((key, [c]))
+    return [ch[1] for ch in chips]
+
+
+def _roles(T, topo):
+    chips = _chips(T, topo)
+    roles = {}
+    for ci, mine in enumerate(chips):
+        other = chips[1 - ci]
+        for die in sorted(set(topo.die(c) for c in mine)):
+            here = [c for c in mine if topo.die(c) == die]
+            far = [c for c in other if topo.die(c) == die]
+            cap = [c for c in here if all(topo.may_write(c, d) for d in other)]
+            non = [c for c in here if c not in cap]
+            if MODE == "direct":
+                for j, c in enumerate(cap):
+                    roles[c] = dict(j=j, chunks=[("far", far[0:2]), ("far", far[2:4])], first=True, via=None)
+                for j, c in enumerate(non):
+                    roles[c] = dict(j=j, chunks=[("near", here[0:2]), ("near", here[2:4])], first=False, via=None)
+            else:
+                world = range(2 * topo.CORES_PER_HOST)
+                helpers = [m for m in world if T.rank_of(m) is None and topo.die(m) == die
+                           and topo.same_plane(here[0], m) and topo.mates(m, far[0])
+                           and all(topo.may_write(m, d) for d in far)]
+                for j, c in enumerate(cap):
+                    roles[c] = dict(j=j, chunks=[("far", far[0:2]), ("near", here[0:2])], first=False, via=None)
+                for j, c in enumerate(non):
+                    roles[c] = dict(j=j, chunks=[("far", far[2:4]), ("near", here[2:4])], first=True, via=helpers[j])
+    return chips, roles
+
+
+def _deliver(topo, c, role):
+    has_far = any(k == "far" for k, _ in role["chunks"])
+    calls = []
+    for ch, (kind, dl) in enumerate(role["chunks"]):
+        tr = []
+        if kind == "far" and role["via"] is not None:
+            tr.append((role["via"], ch * 2 * SW, 2 * SW, _bits(topo.mask(c, role["via"])), "via"))
+        else:
+            for q, d in enumerate(dl):
+                if d == c:
+                    continue
+                es = _bits(topo.mask(c, d))
+                if kind == "near" and has_far:
+                    out = _bits(topo.mask(c, role["via"] if role["via"] is not None else role["chunks"][0][1][0]))
+                    es = [e for e in es if e not in out]
+                h = len(es) // 2
+                tr.append((d, (ch * 2 + q) * SW, SW, es[q * h:(q + 1) * h], kind))
+        calls.append(tr)
+    return calls
+
+
+def _forward(topo, m, keeper, role):
+    dl = [dl for k, dl in role["chunks"] if k == "far"][0]
+    tr = []
+    for q, d in enumerate(dl):
+        es = _bits(topo.mask(m, d))
+        h = len(es) // 2
+        tr.append((d, q * SW, es[q * h:(q + 1) * h]))
+    return tr
+
+
+def _dst(topo, d, c):
+    rid, pid = topo.addr(d, c)
+    return DstId(rid=rid, pnc=pid)
+
+
+def rank_program(g, core, T, topo):
+    chips, roles = _roles(T, topo)
+    sem = T.sem
+    rank = T.rank_of(core)
+
+    if rank is None:
+        mine = [(k, r) for k, r in roles.items() if r["via"] == core]
+        for k, r in mine:
+            g.wait_ge(sem.ar, len(_bits(topo.mask(k, core))))
+            tr = _forward(topo, core, k, r)
+            g.remote_dma_fused(
+                [RemoteDMATransfer(dst_ids=[_dst(topo, d, core)], dma_engine_mask=_mask(es), remote_sem=sem.a2,
+                                   src=T.rel[:, a:a + SW],
+                                   dst=T.win2[:, NB * NCOL + r["j"] * SW:NB * NCOL + (r["j"] + 1) * SW])
+                 for d, a, es in tr], local_sem=sem.ls)
+            g.wait_ge(sem.ls, sum(len(es) for _, _, es in tr))
+        return
+
+    ci = [i for i, ch in enumerate(chips) if core in ch][0]
+    chip = chips[ci]
+    li = chip.index(core)
+    role = roles[core]
+    j = role["j"]
+    V = g.vector
+    nv = [0]
+
+    def vdone(ins):
+        ins.then_inc(sem.v, 1)
+        nv[0] += 1
+
+    def vsync():
+        V.wait_ge(sem.v, nv[0])
+
+    g.sync.dma_start(T.cb[:], T.c[:]).then_inc(sem.ldc, 16)
+    for q in range(8):
+        g.scalar.dma_start(T.par[16 * q:16 * q + 16, :], T.parent[:]).then_inc(sem.ldp, 16)
+
+    g.iota(T.ki[:], [[1, 32]], 0, 16).then_inc(sem.cst, 1)
+    V.wait_ge(sem.cst, 1)
+    vdone(V.tensor_scalar(out=T.ki[:], in0=T.ki[:], scalar1=255, scalar2=None, op0=AluOpType.bitwise_and))
+    vsync()
+    vdone(V.tensor_copy(T.k16[:], T.ki[:, 0:16]))
+    vdone(V.tensor_copy(T.kf[:], T.ki[:]))
+    vsync()
+    vdone(V.transpose(T.kt[:], T.kf[:]))
+
+    V.wait_ge(sem.ldc, 16)
+    V.tensor_copy(T.st[:], T.cb[:].indirect(T.k16[:])).then_inc(sem.dei, 1)
+    vdone(V.tensor_copy(T.win[:, li * SW:(li + 1) * SW], T.cb[:].indirect(T.k16[:, j * W:(j + 1) * W])))
+
+    nls = 0
+    g.wait_ge(sem.dei, 1)
+    for first in (True, False):
+        tr = []
+        for s in range(NS):
+            ds = [k for k in chip if k != core and roles[k]["j"] == s and roles[k]["first"] == first]
+            es = _bits(min(topo.mask(core, k) for k in ds))
+            h = len(es) // NS
+            es = es[s * h:(s + 1) * h]
+            tr.append(RemoteDMATransfer(dst_ids=[_dst(topo, k, core) for k in ds], dma_engine_mask=_mask(es),
+                                        remote_sem=sem.a1, srcs=[T.st[:, s * SW:(s + 1) * SW]],
+                                        dsts=[T.win[:, li * SW:(li + 1) * SW] for k in ds]))
+            nls += len(es)
+        g.remote_dma_fused(tr, local_sem=sem.ls)
+    na1 = 0
+    for k in chip:
+        if k != core:
+            na1 += len(_bits(topo.mask(k, core))) // NS
+
+    V.wait_ge(sem.ldp, 128)
+    vdone(V.tensor_scalar(out=T.pm[:], in0=T.par[:], scalar1=127, scalar2=None, op0=AluOpType.bitwise_and))
+    vdone(V.tensor_scalar(out=T.ph[:], in0=T.par[:], scalar1=112, scalar2=None, op0=AluOpType.bitwise_and))
+    vsync()
+    vdone(V.tensor_scalar(out=T.ph[:], in0=T.ph[:], scalar1=W - 1, scalar2=None, op0=AluOpType.mult))
+    vsync()
+    vdone(V.tensor_tensor(out=T.pb[:], in0=T.pm[:], in1=T.ph[:], op=AluOpType.add))
+    vsync()
+    for c in range(W):
+        vdone(V.tensor_scalar(out=T.of1[:, c::W], in0=T.pb[:], scalar1=16 * c, scalar2=None, op0=AluOpType.add))
+    vsync()
+
+    V.wait_ge(sem.a1, na1)
+    calls = _deliver(topo, core, role)
+    for ch, (kind, dl) in enumerate(role["chunks"]):
+        r0 = T.rank_of(dl[0])
+        assert T.rank_of(dl[1]) == r0 + 1
+        V.tensor_copy(T.sel[:, ch * 2 * SW:(ch + 1) * 2 * SW],
+                      T.win[:].indirect(T.of1[:, r0 * W:(r0 + 2) * W])).then_inc((sem.sa, sem.sb)[ch], 1)
+    for ch, tr in enumerate(calls):
+        g.wait_ge((sem.sa, sem.sb)[ch], 1)
+        lst = []
+        for d, a, n, es, kind in tr:
+            if kind == "via":
+                lst.append(RemoteDMATransfer(dst_ids=[_dst(topo, d, core)], dma_engine_mask=_mask(es),
+                                             remote_sem=sem.ar, src=T.sel[:, a:a + n], dst=T.rel[:]))
+            else:
+                o = (NB * NCOL if kind == "far" else 0) + j * SW
+                lst.append(RemoteDMATransfer(dst_ids=[_dst(topo, d, core)], dma_engine_mask=_mask(es),
+                                             remote_sem=sem.a2, src=T.sel[:, a:a + n], dst=T.win2[:, o:o + SW]))
+            nls += len(es)
+        g.remote_dma_fused(lst, local_sem=sem.ls)
+    if any(kind == "near" and core in dl for kind, dl in role["chunks"]):
+        vdone(V.tensor_copy(T.win2[:, j * SW:(j + 1) * SW], T.win[:].indirect(T.of1[:, rank * W:(rank + 1) * W])))
+
+    half = len(chip) * NB
+    vdone(V.tensor_scalar(out=T.tc[:], in0=T.par[:, rank:rank + 1], scalar1=half, scalar2=NB * NCOL,
+                          op0=(AluOpType.is_ge if ci == 0 else AluOpType.is_lt), op1=AluOpType.mult))
+    vsync()
+    vdone(V.tensor_scalar(out=T.yy[:], in0=T.kt[:], scalar1=T.tc[:, 0:1], scalar2=None, op0=AluOpType.add))
+    vsync()
+    vdone(V.transpose(T.yt[:], T.yy[:]))
+    vsync()
+    vdone(V.tensor_copy(T.of2[:], T.yt[:, 0:16]))
+    vsync()
+
+    na2 = 0
+    for k, r in roles.items():
+        for tr in _deliver(topo, k, r):
+            na2 += sum(len(es) for d, a, n, es, kind in tr if d == core and kind != "via")
+        if r["via"] is not None:
+            na2 += sum(len(es) for d, a, es in _forward(topo, r["via"], k, r) if d == core)
+    V.wait_ge(sem.a2, na2)
+    V.tensor_copy(T.yb[:], T.win2[:].indirect(T.of2[:])).then_inc(sem.fin, 1)
+    g.sync.wait_ge(sem.fin, 1)
+    g.sync.dma_start(T.y[:], T.yb[:]).then_inc(sem.sto, 16)
+
+    g.wait_ge(sem.ls, nls)
+    g.wait_ge(sem.sto, 16)

@@ -1,7 +1,6 @@
 from concourse.bass import DstId, RemoteDMATransfer
-from concourse.mybir import AluOpType
+from concourse.mybir import AluOpType, ActivationFunctionType
 
-MODE = "direct"
 NB, NCOL = 16, 16
 NS = 2
 W = NCOL // NS
@@ -14,7 +13,6 @@ SCRATCH = {
     "sel": ("sbuf", [128, 4 * SW], "float32"),
     "win2": ("sbuf", [128, 2 * NB * NCOL], "float32"),
     "yb": ("sbuf", [128, NB * NCOL], "float32"),
-    "rel": ("sbuf", [128, 2 * SW], "float32"),
     "par": ("sbuf", [128, 16], "int32"),
     "ki": ("sbuf", [128, 32], "int32"),
     "kf": ("sbuf", [128, 32], "float32"),
@@ -29,7 +27,8 @@ SCRATCH = {
     "yt": ("sbuf", [128, 32], "float32"),
     "of2": ("sbuf", [128, 16], "uint16"),
 }
-SEMAPHORES = ["ldc", "ldp", "cst", "v", "dei", "sa", "sb", "a1", "a2", "ar", "ls", "fin", "sto"]
+SEMAPHORES = ["ldc", "ldp", "cst", "v", "kr", "d0", "d1", "o1", "o2", "s0", "s1", "s2", "s3", "a1", "a2", "ls", "fin",
+              "sto"]
 
 
 def _bits(m):
@@ -62,52 +61,44 @@ def _roles(T, topo):
             far = [c for c in other if topo.die(c) == die]
             cap = [c for c in here if all(topo.may_write(c, d) for d in other)]
             non = [c for c in here if c not in cap]
-            if MODE == "direct":
-                for j, c in enumerate(cap):
-                    roles[c] = dict(j=j, chunks=[("far", far[0:2]), ("far", far[2:4])], first=True, via=None)
-                for j, c in enumerate(non):
-                    roles[c] = dict(j=j, chunks=[("near", here[0:2]), ("near", here[2:4])], first=False, via=None)
-            else:
-                world = range(2 * topo.CORES_PER_HOST)
-                helpers = [m for m in world if T.rank_of(m) is None and topo.die(m) == die
-                           and topo.same_plane(here[0], m) and topo.mates(m, far[0])
-                           and all(topo.may_write(m, d) for d in far)]
-                for j, c in enumerate(cap):
-                    roles[c] = dict(j=j, chunks=[("far", far[0:2]), ("near", here[0:2])], first=False, via=None)
-                for j, c in enumerate(non):
-                    roles[c] = dict(j=j, chunks=[("far", far[2:4]), ("near", here[2:4])], first=True, via=helpers[j])
+            for j, c in enumerate(cap):
+                roles[c] = dict(j=j, chunks=[("far", far[0:2]), ("far", far[2:4])], first=True)
+            for j, c in enumerate(non):
+                roles[c] = dict(j=j, chunks=[("near", here[0:2]), ("near", here[2:4])], first=False)
     return chips, roles
 
 
-def _deliver(topo, c, role):
-    has_far = any(k == "far" for k, _ in role["chunks"])
+def _spread(topo, chip, roles, c):
+    es = _bits(min(topo.mask(c, k) for k in chip if k != c))
+    far = [d for kind, dl in roles[c]["chunks"] for d in dl if kind == "far"]
+    low = [e for e in es if far and e in _bits(topo.mask(c, far[0]))]
+    if len(low) != len(es) // NS:
+        low = es[:len(es) // NS]
+    high = [e for e in es if e not in low]
+    half = {roles[c]["j"]: low, 1 - roles[c]["j"]: high}
     calls = []
-    for ch, (kind, dl) in enumerate(role["chunks"]):
+    for first in (True, False):
         tr = []
-        if kind == "far" and role["via"] is not None:
-            tr.append((role["via"], ch * 2 * SW, 2 * SW, _bits(topo.mask(c, role["via"])), "via"))
-        else:
-            for q, d in enumerate(dl):
-                if d == c:
-                    continue
-                es = _bits(topo.mask(c, d))
-                if kind == "near" and has_far:
-                    out = _bits(topo.mask(c, role["via"] if role["via"] is not None else role["chunks"][0][1][0]))
-                    es = [e for e in es if e not in out]
-                h = len(es) // 2
-                tr.append((d, (ch * 2 + q) * SW, SW, es[q * h:(q + 1) * h], kind))
-        calls.append(tr)
+        for s in range(NS):
+            ds = [k for k in chip if k != c and roles[k]["j"] == s and roles[k]["first"] == first]
+            ds.sort(key=lambda k: topo.die(k) != topo.die(c))
+            n = len(ds)
+            one = [(s, k, half[s][i::n]) for i, k in enumerate(ds)]
+            if first:
+                calls.append(one)
+            else:
+                tr += one
+        if not first:
+            calls.append(tr)
     return calls
 
 
-def _forward(topo, m, keeper, role):
-    dl = [dl for k, dl in role["chunks"] if k == "far"][0]
-    tr = []
-    for q, d in enumerate(dl):
-        es = _bits(topo.mask(m, d))
-        h = len(es) // 2
-        tr.append((d, q * SW, es[q * h:(q + 1) * h]))
-    return tr
+def _deliver(topo, c, role):
+    calls = []
+    for ch, (kind, dl) in enumerate(role["chunks"]):
+        for q, d in enumerate(dl):
+            calls.append((d, (ch * 2 + q) * SW, _bits(topo.mask(c, d)) if d != c else [], kind))
+    return calls
 
 
 def _dst(topo, d, c):
@@ -116,29 +107,18 @@ def _dst(topo, d, c):
 
 
 def rank_program(g, core, T, topo):
-    chips, roles = _roles(T, topo)
     sem = T.sem
     rank = T.rank_of(core)
-
     if rank is None:
-        mine = [(k, r) for k, r in roles.items() if r["via"] == core]
-        for k, r in mine:
-            g.wait_ge(sem.ar, len(_bits(topo.mask(k, core))))
-            tr = _forward(topo, core, k, r)
-            g.remote_dma_fused(
-                [RemoteDMATransfer(dst_ids=[_dst(topo, d, core)], dma_engine_mask=_mask(es), remote_sem=sem.a2,
-                                   src=T.rel[:, a:a + SW],
-                                   dst=T.win2[:, NB * NCOL + r["j"] * SW:NB * NCOL + (r["j"] + 1) * SW])
-                 for d, a, es in tr], local_sem=sem.ls)
-            g.wait_ge(sem.ls, sum(len(es) for _, _, es in tr))
         return
-
+    chips, roles = _roles(T, topo)
     ci = [i for i, ch in enumerate(chips) if core in ch][0]
     chip = chips[ci]
     li = chip.index(core)
     role = roles[core]
     j = role["j"]
     V = g.vector
+    S = g.scalar
     nv = [0]
 
     def vdone(ins):
@@ -148,41 +128,52 @@ def rank_program(g, core, T, topo):
     def vsync():
         V.wait_ge(sem.v, nv[0])
 
+    def gather(q, out, win, off):
+        if q == 0:
+            return V.tensor_copy(out, win.indirect(off))
+        return S.activation(out, win.indirect(off), ActivationFunctionType.Copy)
+
+    def both(s, n):
+        V.wait_ge(s, n)
+        S.wait_ge(s, n)
+
     g.sync.dma_start(T.cb[:], T.c[:]).then_inc(sem.ldc, 16)
     for q in range(8):
-        g.scalar.dma_start(T.par[16 * q:16 * q + 16, :], T.parent[:]).then_inc(sem.ldp, 16)
+        g.sync.dma_start(T.par[16 * q:16 * q + 16, :], T.parent[:]).then_inc(sem.ldp, 16)
 
     g.iota(T.ki[:], [[1, 32]], 0, 16).then_inc(sem.cst, 1)
     V.wait_ge(sem.cst, 1)
     vdone(V.tensor_scalar(out=T.ki[:], in0=T.ki[:], scalar1=255, scalar2=None, op0=AluOpType.bitwise_and))
     vsync()
-    vdone(V.tensor_copy(T.k16[:], T.ki[:, 0:16]))
+    V.tensor_copy(T.k16[:], T.ki[:, 0:16]).then_inc(sem.kr, 1)
     vdone(V.tensor_copy(T.kf[:], T.ki[:]))
     vsync()
     vdone(V.transpose(T.kt[:], T.kf[:]))
 
-    V.wait_ge(sem.ldc, 16)
-    V.tensor_copy(T.st[:], T.cb[:].indirect(T.k16[:])).then_inc(sem.dei, 1)
-    vdone(V.tensor_copy(T.win[:, li * SW:(li + 1) * SW], T.cb[:].indirect(T.k16[:, j * W:(j + 1) * W])))
+    both(sem.kr, 1)
+    both(sem.ldc, 16)
+    src = []
+    hw = W // 2
+    for s in range(NS):
+        o, buf = (li * SW, T.win) if s == j else (s * SW, T.st)
+        for q in range(2):
+            gather(q, buf[:, o + q * hw * NB:o + (q + 1) * hw * NB], T.cb[:],
+                   T.k16[:, s * W + q * hw:s * W + (q + 1) * hw]).then_inc(sem["d%d" % s], 1)
+        src.append(buf[:, o:o + SW])
 
     nls = 0
-    g.wait_ge(sem.dei, 1)
-    for first in (True, False):
-        tr = []
-        for s in range(NS):
-            ds = [k for k in chip if k != core and roles[k]["j"] == s and roles[k]["first"] == first]
-            es = _bits(min(topo.mask(core, k) for k in ds))
-            h = len(es) // NS
-            es = es[s * h:(s + 1) * h]
-            tr.append(RemoteDMATransfer(dst_ids=[_dst(topo, k, core) for k in ds], dma_engine_mask=_mask(es),
-                                        remote_sem=sem.a1, srcs=[T.st[:, s * SW:(s + 1) * SW]],
-                                        dsts=[T.win[:, li * SW:(li + 1) * SW] for k in ds]))
-            nls += len(es)
-        g.remote_dma_fused(tr, local_sem=sem.ls)
+    for n, call in enumerate(_spread(topo, chip, roles, core)):
+        if n < NS:
+            g.wait_ge(sem["d%d" % call[0][0]], 2)
+        g.remote_dma_fused(
+            [RemoteDMATransfer(dst_ids=[_dst(topo, k, core)], dma_engine_mask=_mask(es), remote_sem=sem.a1,
+                               src=src[s], dst=T.win[:, li * SW:(li + 1) * SW]) for s, k, es in call],
+            local_sem=sem.ls)
+        nls += sum(len(es) for s, k, es in call)
     na1 = 0
     for k in chip:
-        if k != core:
-            na1 += len(_bits(topo.mask(k, core))) // NS
+        for call in _spread(topo, chip, roles, k):
+            na1 += sum(len(es) for s, d, es in call if d == core)
 
     V.wait_ge(sem.ldp, 128)
     vdone(V.tensor_scalar(out=T.pm[:], in0=T.par[:], scalar1=127, scalar2=None, op0=AluOpType.bitwise_and))
@@ -193,31 +184,28 @@ def rank_program(g, core, T, topo):
     vdone(V.tensor_tensor(out=T.pb[:], in0=T.pm[:], in1=T.ph[:], op=AluOpType.add))
     vsync()
     for c in range(W):
-        vdone(V.tensor_scalar(out=T.of1[:, c::W], in0=T.pb[:], scalar1=16 * c, scalar2=None, op0=AluOpType.add))
-    vsync()
+        V.tensor_scalar(out=T.of1[:, c::W], in0=T.pb[:], scalar1=16 * c, scalar2=None,
+                        op0=AluOpType.add).then_inc(sem.o1, 1)
 
-    V.wait_ge(sem.a1, na1)
-    calls = _deliver(topo, core, role)
-    for ch, (kind, dl) in enumerate(role["chunks"]):
-        r0 = T.rank_of(dl[0])
-        assert T.rank_of(dl[1]) == r0 + 1
-        V.tensor_copy(T.sel[:, ch * 2 * SW:(ch + 1) * 2 * SW],
-                      T.win[:].indirect(T.of1[:, r0 * W:(r0 + 2) * W])).then_inc((sem.sa, sem.sb)[ch], 1)
-    for ch, tr in enumerate(calls):
-        g.wait_ge((sem.sa, sem.sb)[ch], 1)
-        lst = []
-        for d, a, n, es, kind in tr:
-            if kind == "via":
-                lst.append(RemoteDMATransfer(dst_ids=[_dst(topo, d, core)], dma_engine_mask=_mask(es),
-                                             remote_sem=sem.ar, src=T.sel[:, a:a + n], dst=T.rel[:]))
-            else:
-                o = (NB * NCOL if kind == "far" else 0) + j * SW
-                lst.append(RemoteDMATransfer(dst_ids=[_dst(topo, d, core)], dma_engine_mask=_mask(es),
-                                             remote_sem=sem.a2, src=T.sel[:, a:a + n], dst=T.win2[:, o:o + SW]))
-            nls += len(es)
-        g.remote_dma_fused(lst, local_sem=sem.ls)
-    if any(kind == "near" and core in dl for kind, dl in role["chunks"]):
-        vdone(V.tensor_copy(T.win2[:, j * SW:(j + 1) * SW], T.win[:].indirect(T.of1[:, rank * W:(rank + 1) * W])))
+    both(sem.o1, W)
+    both(sem["d%d" % j], 2)
+    both(sem.a1, na1)
+    plan = _deliver(topo, core, role)
+    for n, (d, a, es, kind) in enumerate(plan):
+        r = T.rank_of(d)
+        o, buf = (j * SW, T.win2) if d == core else (a, T.sel)
+        for q in range(2):
+            gather(q, buf[:, o + q * hw * NB:o + (q + 1) * hw * NB], T.win[:],
+                   T.of1[:, r * W + q * hw:r * W + (q + 1) * hw]).then_inc(sem["s%d" % n], 1)
+    for n, (d, a, es, kind) in enumerate(plan):
+        g.wait_ge(sem["s%d" % n], 2)
+        if d == core:
+            continue
+        o = (NB * NCOL if kind == "far" else 0) + j * SW
+        g.remote_dma_fused(
+            [RemoteDMATransfer(dst_ids=[_dst(topo, d, core)], dma_engine_mask=_mask(es), remote_sem=sem.a2,
+                               src=T.sel[:, a:a + SW], dst=T.win2[:, o:o + SW])], local_sem=sem.ls)
+        nls += len(es)
 
     half = len(chip) * NB
     vdone(V.tensor_scalar(out=T.tc[:], in0=T.par[:, rank:rank + 1], scalar1=half, scalar2=NB * NCOL,
@@ -227,18 +215,20 @@ def rank_program(g, core, T, topo):
     vsync()
     vdone(V.transpose(T.yt[:], T.yy[:]))
     vsync()
-    vdone(V.tensor_copy(T.of2[:], T.yt[:, 0:16]))
-    vsync()
+    V.tensor_copy(T.of2[:], T.yt[:, 0:16]).then_inc(sem.o2, 1)
 
     na2 = 0
     for k, r in roles.items():
-        for tr in _deliver(topo, k, r):
-            na2 += sum(len(es) for d, a, n, es, kind in tr if d == core and kind != "via")
-        if r["via"] is not None:
-            na2 += sum(len(es) for d, a, es in _forward(topo, r["via"], k, r) if d == core)
-    V.wait_ge(sem.a2, na2)
-    V.tensor_copy(T.yb[:], T.win2[:].indirect(T.of2[:])).then_inc(sem.fin, 1)
-    g.sync.wait_ge(sem.fin, 1)
+        na2 += sum(len(es) for d, a, es, kind in _deliver(topo, k, r) if d == core)
+    both(sem.o2, 1)
+    for n in range(len(plan)):
+        both(sem["s%d" % n], 2)
+    both(sem.a2, na2)
+    hs = NB // 2
+    for q in range(2):
+        gather(q, T.yb[:, q * hs * NCOL:(q + 1) * hs * NCOL], T.win2[:],
+               T.of2[:, q * hs:(q + 1) * hs]).then_inc(sem.fin, 1)
+    g.sync.wait_ge(sem.fin, 2)
     g.sync.dma_start(T.y[:], T.yb[:]).then_inc(sem.sto, 16)
 
     g.wait_ge(sem.ls, nls)

from concourse.bass import DstId, RemoteDMATransfer
from concourse.mybir import AluOpType, ActivationFunctionType

NB, NCOL = 16, 16
NS = 2
W = NCOL // NS
SW = NB * W

SCRATCH = {
    "cb": ("sbuf", [128, NB * NCOL], "float32"),
    "st": ("sbuf", [128, NB * NCOL], "float32"),
    "win": ("sbuf", [128, 8 * SW], "float32"),
    "sel": ("sbuf", [128, 4 * SW], "float32"),
    "win2": ("sbuf", [128, 2 * NB * NCOL], "float32"),
    "yb": ("sbuf", [128, NB * NCOL], "float32"),
    "par": ("sbuf", [128, 16], "int32"),
    "ki": ("sbuf", [128, 32], "int32"),
    "kf": ("sbuf", [128, 32], "float32"),
    "kt": ("sbuf", [128, 32], "float32"),
    "k16": ("sbuf", [128, 16], "uint16"),
    "pm": ("sbuf", [128, 16], "int32"),
    "ph": ("sbuf", [128, 16], "int32"),
    "pb": ("sbuf", [128, 16], "int32"),
    "of1": ("sbuf", [128, 16 * W], "uint16"),
    "tc": ("sbuf", [128, 1], "float32"),
    "yy": ("sbuf", [128, 32], "float32"),
    "yt": ("sbuf", [128, 32], "float32"),
    "of2": ("sbuf", [128, 16], "uint16"),
}
SEMAPHORES = ["ldc", "ldp", "cst", "v", "kr", "d0", "d1", "o1", "o2", "s0", "s1", "s2", "s3", "a1", "a2", "ls", "fin",
              "sto"]


def _bits(m):
    return [e for e in range(16) if (m >> e) & 1]


def _mask(es):
    return sum(1 << e for e in es)


def _chips(T, topo):
    chips = []
    for c in T.cores:
        key = (topo.host(c), topo.chip(c))
        hit = [ch for ch in chips if ch[0] == key]
        if hit:
            hit[0][1].append(c)
        else:
            chips.append((key, [c]))
    return [ch[1] for ch in chips]


def _roles(T, topo):
    chips = _chips(T, topo)
    roles = {}
    for ci, mine in enumerate(chips):
        other = chips[1 - ci]
        for die in sorted(set(topo.die(c) for c in mine)):
            here = [c for c in mine if topo.die(c) == die]
            far = [c for c in other if topo.die(c) == die]
            cap = [c for c in here if all(topo.may_write(c, d) for d in other)]
            non = [c for c in here if c not in cap]
            for j, c in enumerate(cap):
                roles[c] = dict(j=j, chunks=[("far", far[0:2]), ("far", far[2:4])], first=True)
            for j, c in enumerate(non):
                roles[c] = dict(j=j, chunks=[("near", here[0:2]), ("near", here[2:4])], first=False)
    return chips, roles


def _spread(topo, chip, roles, c):
    es = _bits(min(topo.mask(c, k) for k in chip if k != c))
    far = [d for kind, dl in roles[c]["chunks"] for d in dl if kind == "far"]
    low = [e for e in es if far and e in _bits(topo.mask(c, far[0]))]
    if len(low) != len(es) // NS:
        low = es[:len(es) // NS]
    high = [e for e in es if e not in low]
    half = {roles[c]["j"]: low, 1 - roles[c]["j"]: high}
    calls = []
    for first in (True, False):
        tr = []
        for s in range(NS):
            ds = [k for k in chip if k != c and roles[k]["j"] == s and roles[k]["first"] == first]
            ds.sort(key=lambda k: topo.die(k) != topo.die(c))
            n = len(ds)
            one = [(s, k, half[s][i::n]) for i, k in enumerate(ds)]
            if first:
                calls.append(one)
            else:
                tr += one
        if not first:
            calls.append(tr)
    return calls


def _deliver(topo, c, role):
    calls = []
    for ch, (kind, dl) in enumerate(role["chunks"]):
        for q, d in enumerate(dl):
            calls.append((d, (ch * 2 + q) * SW, _bits(topo.mask(c, d)) if d != c else [], kind))
    return calls


def _dst(topo, d, c):
    rid, pid = topo.addr(d, c)
    return DstId(rid=rid, pnc=pid)


def rank_program(g, core, T, topo):
    sem = T.sem
    rank = T.rank_of(core)
    if rank is None:
        return
    chips, roles = _roles(T, topo)
    ci = [i for i, ch in enumerate(chips) if core in ch][0]
    chip = chips[ci]
    li = chip.index(core)
    role = roles[core]
    j = role["j"]
    V = g.vector
    S = g.scalar
    nv = [0]

    def vdone(ins):
        ins.then_inc(sem.v, 1)
        nv[0] += 1

    def vsync():
        V.wait_ge(sem.v, nv[0])

    def gather(q, out, win, off):
        if q == 0:
            return V.tensor_copy(out, win.indirect(off))
        return S.activation(out, win.indirect(off), ActivationFunctionType.Copy)

    def both(s, n):
        V.wait_ge(s, n)
        S.wait_ge(s, n)

    g.sync.dma_start(T.cb[:], T.c[:]).then_inc(sem.ldc, 16)
    for q in range(8):
        g.sync.dma_start(T.par[16 * q:16 * q + 16, :], T.parent[:]).then_inc(sem.ldp, 16)

    g.iota(T.ki[:], [[1, 32]], 0, 16).then_inc(sem.cst, 1)
    V.wait_ge(sem.cst, 1)
    vdone(V.tensor_scalar(out=T.ki[:], in0=T.ki[:], scalar1=255, scalar2=None, op0=AluOpType.bitwise_and))
    vsync()
    V.tensor_copy(T.k16[:], T.ki[:, 0:16]).then_inc(sem.kr, 1)
    vdone(V.tensor_copy(T.kf[:], T.ki[:]))
    vsync()
    vdone(V.transpose(T.kt[:], T.kf[:]))

    both(sem.kr, 1)
    both(sem.ldc, 16)
    src = []
    hw = W // 2
    for s in range(NS):
        o, buf = (li * SW, T.win) if s == j else (s * SW, T.st)
        for q in range(2):
            gather(q, buf[:, o + q * hw * NB:o + (q + 1) * hw * NB], T.cb[:],
                   T.k16[:, s * W + q * hw:s * W + (q + 1) * hw]).then_inc(sem["d%d" % s], 1)
        src.append(buf[:, o:o + SW])

    nls = 0
    for n, call in enumerate(_spread(topo, chip, roles, core)):
        if n < NS:
            g.wait_ge(sem["d%d" % call[0][0]], 2)
        g.remote_dma_fused(
            [RemoteDMATransfer(dst_ids=[_dst(topo, k, core)], dma_engine_mask=_mask(es), remote_sem=sem.a1,
                               src=src[s], dst=T.win[:, li * SW:(li + 1) * SW]) for s, k, es in call],
            local_sem=sem.ls)
        nls += sum(len(es) for s, k, es in call)
    na1 = 0
    for k in chip:
        for call in _spread(topo, chip, roles, k):
            na1 += sum(len(es) for s, d, es in call if d == core)

    V.wait_ge(sem.ldp, 128)
    vdone(V.tensor_scalar(out=T.pm[:], in0=T.par[:], scalar1=127, scalar2=None, op0=AluOpType.bitwise_and))
    vdone(V.tensor_scalar(out=T.ph[:], in0=T.par[:], scalar1=112, scalar2=None, op0=AluOpType.bitwise_and))
    vsync()
    vdone(V.tensor_scalar(out=T.ph[:], in0=T.ph[:], scalar1=W - 1, scalar2=None, op0=AluOpType.mult))
    vsync()
    vdone(V.tensor_tensor(out=T.pb[:], in0=T.pm[:], in1=T.ph[:], op=AluOpType.add))
    vsync()
    for c in range(W):
        V.tensor_scalar(out=T.of1[:, c::W], in0=T.pb[:], scalar1=16 * c, scalar2=None,
                        op0=AluOpType.add).then_inc(sem.o1, 1)

    both(sem.o1, W)
    both(sem["d%d" % j], 2)
    both(sem.a1, na1)
    plan = _deliver(topo, core, role)
    for n, (d, a, es, kind) in enumerate(plan):
        r = T.rank_of(d)
        o, buf = (j * SW, T.win2) if d == core else (a, T.sel)
        for q in range(2):
            gather(q, buf[:, o + q * hw * NB:o + (q + 1) * hw * NB], T.win[:],
                   T.of1[:, r * W + q * hw:r * W + (q + 1) * hw]).then_inc(sem["s%d" % n], 1)
    for n, (d, a, es, kind) in enumerate(plan):
        g.wait_ge(sem["s%d" % n], 2)
        if d == core:
            continue
        o = (NB * NCOL if kind == "far" else 0) + j * SW
        g.remote_dma_fused(
            [RemoteDMATransfer(dst_ids=[_dst(topo, d, core)], dma_engine_mask=_mask(es), remote_sem=sem.a2,
                               src=T.sel[:, a:a + SW], dst=T.win2[:, o:o + SW])], local_sem=sem.ls)
        nls += len(es)

    half = len(chip) * NB
    vdone(V.tensor_scalar(out=T.tc[:], in0=T.par[:, rank:rank + 1], scalar1=half, scalar2=NB * NCOL,
                          op0=(AluOpType.is_ge if ci == 0 else AluOpType.is_lt), op1=AluOpType.mult))
    vsync()
    vdone(V.tensor_scalar(out=T.yy[:], in0=T.kt[:], scalar1=T.tc[:, 0:1], scalar2=None, op0=AluOpType.add))
    vsync()
    vdone(V.transpose(T.yt[:], T.yy[:]))
    vsync()
    V.tensor_copy(T.of2[:], T.yt[:, 0:16]).then_inc(sem.o2, 1)

    na2 = 0
    for k, r in roles.items():
        na2 += sum(len(es) for d, a, es, kind in _deliver(topo, k, r) if d == core)
    both(sem.o2, 1)
    for n in range(len(plan)):
        both(sem["s%d" % n], 2)
    both(sem.a2, na2)
    hs = NB // 2
    for q in range(2):
        gather(q, T.yb[:, q * hs * NCOL:(q + 1) * hs * NCOL], T.win2[:],
               T.of2[:, q * hs:(q + 1) * hs]).then_inc(sem.fin, 1)
    g.sync.wait_ge(sem.fin, 2)
    g.sync.dma_start(T.y[:], T.yb[:]).then_inc(sem.sto, 16)

    g.wait_ge(sem.ls, nls)
    g.wait_ge(sem.sto, 16)
